import numpy as np
import ml_dtypes


def mxq(x, axis, fmt="e4m3"):
    dtype, down = {"e4m3": (ml_dtypes.float8_e4m3fn, 7), "e5m2": (ml_dtypes.float8_e5m2, 14)}[fmt]
    v = np.moveaxis(np.asarray(x, np.float32).astype(ml_dtypes.bfloat16).astype(np.float64), axis, -1)
    blocks = v.reshape(v.shape[:-1] + (-1, 32))
    amax = np.abs(blocks).max(-1, keepdims=True)
    byte = np.maximum(np.where(amax > 0, np.frexp(amax)[1] - 1 + 127, 0) - down, 1)
    scale = np.exp2(byte - 127.0)
    codes = (blocks / scale).astype(np.float32).astype(dtype).astype(np.float64)
    return np.moveaxis((codes * scale).reshape(v.shape), -1, axis)


WIDE = False


def mx_kscale(k):
    if not WIDE:
        return np.ones(k)
    levels = np.array([10, -10, 5, -5, 0])
    if k % 512:
        return np.exp2(np.random.permutation(np.resize(levels, k // 32))).repeat(32)
    a = np.empty((k // 512, 16))
    for p in range(k // 512):
        a[p, :8] = np.random.permutation(np.resize(levels, 8))
        for g in range(8):
            far = levels[np.abs(levels - a[p, g]) >= 10]
            a[p, g + 8] = far[np.random.randint(len(far))]
    return np.exp2(a.ravel()).repeat(32)


def f64(x):
    return np.asarray(x).astype(np.float64)


def striped(idx):
    return np.tile(np.asarray(idx).reshape(-1, 16).T, (8, 1)).astype(np.uint16)


def unstriped(offs):
    return offs[:16].T.reshape(-1).astype(np.int64)


def striped8(idx):
    return np.asarray(idx).reshape(8, -1, 16).transpose(0, 2, 1).reshape(128, -1).astype(np.uint16)


def unstriped8(offs):
    return offs.reshape(8, 16, -1).transpose(0, 2, 1).reshape(8, -1).astype(np.int64)


def pick8(x, idx, run):
    r = np.arange(len(x))
    return x[r[:, None], idx[r % (8 * run) // run]]


E2M1 = np.array([0.0, 0.5, 1.0, 1.5, 2.0, 3.0, 4.0, 6.0, -0.0, -0.5, -1.0, -1.5, -2.0, -3.0, -4.0, -6.0])


def pack_weight(w, fmt):
    k, n = w.shape
    w = f64(np.asarray(w, np.float32).astype(ml_dtypes.bfloat16)).reshape(k // 32, 32, n)
    amax = np.abs(w).max(1)
    if fmt == "e4m3":
        byte = np.frexp(amax)[1] - 1 + 127 - 7
    else:
        mant, ex = np.frexp(amax / 6.0)
        byte = np.where(mant > 0.5, ex, ex - 1) + 127
    byte = np.clip(np.where(amax > 0, byte, 1), 1, 254)
    scaled = (w * np.exp2(127.0 - byte)[:, None, :]).reshape(k, n).astype(np.float32)
    by_word = np.ascontiguousarray(scaled.reshape(k // 512, 128, 4, n).transpose(0, 1, 3, 2))
    if fmt == "e4m3":
        words = by_word.astype(ml_dtypes.float8_e4m3fn).view(np.uint8)
    else:
        c = by_word.astype(ml_dtypes.float4_e2m1fn).view(np.uint8) & 0xF
        words = (c[..., 0::2] | (c[..., 1::2] << 4)).reshape(k // 512, 128, 2 * n)
    return np.ascontiguousarray(words), np.ascontiguousarray(byte.astype(np.uint8).reshape(k // 512, 16, n))


def unpack_weight(words, scales, fmt):
    g, _, n = scales.shape
    words = np.ascontiguousarray(words).reshape(g, 128, n, -1)
    if fmt == "e4m3":
        vals = words.view(ml_dtypes.float8_e4m3fn).astype(np.float64)
    else:
        nib = np.empty((g, 128, n, 4), np.uint8)
        nib[..., 0::2] = words & 0xF
        nib[..., 1::2] = words >> 4
        vals = E2M1[nib]
    vals = vals * np.repeat(np.exp2(scales.astype(np.float64) - 127.0), 8, axis=1)[..., None]
    return vals.transpose(0, 1, 3, 2).reshape(g * 512, n)


K, J, R, T, Z, M, O, S, C, N = 512, 512, 512, 1024, 512, 1024, 256, 256, 512, 256


def setup_inputs():
    n = np.random.standard_normal
    idx = np.random.permutation(T)[:J]
    idx2 = np.random.permutation(M)[:J]
    idx3 = np.stack([np.random.permutation(J)[:S] for _ in range(8)])
    idx4 = np.stack([np.random.permutation(C)[:S] for _ in range(8)])
    idx5 = np.stack([np.random.permutation(C)[:S] for _ in range(8)])
    idx6 = np.stack([np.random.permutation(C)[:S] for _ in range(8)])
    idx7 = np.stack([np.random.permutation(C)[:O] for _ in range(8)])
    fk = mx_kscale(K)
    fr = mx_kscale(R)
    fz = mx_kscale(Z)
    xtp = pack_weight(n((K, T)) * fk[:, None], "e2m1")
    wp = pack_weight(n((K, R)) * 1 / np.sqrt(K) / fk[:, None] * fr, "e4m3")
    xop = pack_weight(n((Z, M)) / fz[:, None], "e4m3")
    w2p = pack_weight(n((Z, R)) * 1 / np.sqrt(Z) * fz[:, None] * fr, "e2m1")
    wbp = pack_weight(n((R, N)) * 1 / np.sqrt(R) / fr[:, None], "e2m1")
    return {
        "xt_words": xtp[0],
        "xt_scales": xtp[1],
        "w_words": wp[0],
        "w_scales": wp[1],
        "xo_words": xop[0],
        "xo_scales": xop[1],
        "w2_words": w2p[0],
        "w2_scales": w2p[1],
        "sa": (np.random.uniform(0.5, 1.6, (R, 1))).astype(np.float32),
        "sb": (np.random.uniform(0.5, 1.6, (R, 1))).astype(np.float32),
        "wb_words": wbp[0],
        "wb_scales": wbp[1],
        "offs": striped(idx),
        "offs2": striped(idx2),
        "offs3": striped8(idx3),
        "offs4": striped8(idx4),
        "offs5": striped8(idx5),
        "offs6": striped8(idx6),
        "offs7": striped8(idx7),
    }


def reference(xt_words, xt_scales, w_words, w_scales, xo_words, xo_scales, w2_words, w2_scales, sa, sb, wb_words, wb_scales, offs, offs2, offs3, offs4, offs5, offs6, offs7):
    idx = unstriped(offs)
    idx2 = unstriped(offs2)
    idx3 = unstriped8(offs3)
    idx4 = unstriped8(offs4)
    idx5 = unstriped8(offs5)
    idx6 = unstriped8(offs6)
    idx7 = unstriped8(offs7)
    xtu = unpack_weight(xt_words, xt_scales, "e2m1")
    wu = unpack_weight(w_words, w_scales, "e4m3")
    xou = unpack_weight(xo_words, xo_scales, "e4m3")
    w2u = unpack_weight(w2_words, w2_scales, "e2m1")
    wbu = unpack_weight(wb_words, wb_scales, "e2m1")
    xtidxg = xtu[:, idx]
    xoidx2g = xou[:, idx2]
    a = wu.T @ xtidxg + w2u.T @ xoidx2g
    h1 = pick8(a, idx3, 64) * f64(sa)
    pw = np.zeros((R, C))
    pw[np.arange(R)[:, None], idx4[np.arange(R) % 512 // 64]] = h1
    pv = np.zeros((R, C))
    pv[np.arange(R)[:, None], idx5[np.arange(R) % 512 // 64]] = h1
    pu = np.zeros((R, C))
    pu[np.arange(R)[:, None], idx6[np.arange(R) % 512 // 64]] = h1
    g1 = np.maximum(pw + pv - pu, 0.0)
    hid = pick8(g1, idx7, 64) * f64(sb)
    hidq = mxq(hid, 0, "e4m3")
    y = wbu.T @ hidq
    return y

@@ -1,0 +1,199 @@
+from contextlib import ExitStack
+
+import concourse.mybir as mybir
+
+F32 = mybir.dt.float32
+BF16 = mybir.dt.bfloat16
+I32 = mybir.dt.int32
+U32 = mybir.dt.uint32
+U16 = mybir.dt.uint16
+U8 = mybir.dt.uint8
+FP8X4 = mybir.dt.float8_e4m3fn_x4
+FP4X4 = mybir.dt.float4_e2m1fn_x4
+ALU = mybir.AluOpType
+COPY = mybir.ActivationFunctionType.Copy
+
+K, J, R, T, Z, M, O, S, C, N = 512, 512, 512, 1024, 512, 1024, 256, 256, 512, 256
+P = 128
+PACK = 4
+HALF = 256
+FLOPS = 2 * (K * R * J + Z * R * J + R * N * O)
+
+
+def tile_picked_tokens_plain_bank_threeposts_one_plain_kernel(
+    tc, xt_words, xt_scales, w_words, w_scales, xo_words, xo_scales, w2_words, w2_scales, sa, sb,
+    wb_words, wb_scales, offs, offs2, offs3, offs4, offs5, offs6, offs7, out,
+):
+    nc = tc.nc
+    with ExitStack() as ctx:
+        lists = ctx.enter_context(tc.tile_pool(name="lists", bufs=1))
+        keep = ctx.enter_context(tc.tile_pool(name="keep", bufs=1))
+        psum = ctx.enter_context(tc.psum_pool(name="psum", bufs=1))
+
+        def sb_tile(name, shape, dtype, **kw):
+            return keep.tile(shape, dtype, name=name, align_bytes=64, **kw)
+
+        def load_list(name, src):
+            tile = lists.tile(list(src.shape), U16, name=name)
+            nc.sync.dma_start(tile[:], src)
+            return tile
+
+        def zeroed_plane(name, width):
+            plane = sb_tile(name, [P, width], U8)
+            nc.vector.memset(plane[:].bitcast(I32), 0)
+            return plane
+
+        def load_scale_rows(queue, plane, src):
+            for q in range(4):
+                queue.dma_start(plane[32 * q : 32 * q + 4, :].bitcast(I32), src[0, 4 * q : 4 * q + 4, :].bitcast(I32))
+
+        def load_words(name, src, nbytes):
+            tile = sb_tile(name, [P, nbytes], U8)
+            nc.sync.dma_start(tile[:].bitcast(I32), src.bitcast(I32))
+            return tile
+
+        xt_plane = zeroed_plane("xt_plane", T)
+        w_stage = sb_tile("w_stage", [P, 4, 2 * R], U8)
+        nc.vector.memset(w_stage[:, 0, :].bitcast(I32), 0)
+        xo_plane = zeroed_plane("xo_plane", M)
+        boards = []
+        for name in ("pw", "pv", "pu"):
+            board = sb_tile(name, [P, C], F32)
+            nc.vector.memset(board[:], 0.0)
+            boards.append(board)
+        pw, pv, pu = boards
+        wb_plane = zeroed_plane("wb_plane", N)
+
+        tok_list = load_list("tok_list", offs)
+        xt_table = load_words("xt_table", xt_words[0], 2 * T)
+        load_scale_rows(nc.sync, xt_plane, xt_scales)
+        note_list = load_list("note_list", offs2)
+        xo_table = load_words("xo_table", xo_words[0].rearrange("p c b -> p (c b)"), 4 * M)
+        for which, src in enumerate((w_scales, w2_scales)):
+            nc.sync.dma_start(
+                w_stage[0:4, :, R * which : R * (which + 1)].bitcast(I32),
+                src[0].rearrange("(q i) c -> i q c", i=4).bitcast(I32),
+            )
+        w_raw = load_words("w_raw", w_words[0].rearrange("p c b -> p (c b)"), 4 * R)
+        w2_raw = load_words("w2_raw", w2_words[0], 2 * R)
+        load_scale_rows(nc.sync, xo_plane, xo_scales)
+        seat_list = load_list("seat_list", offs3)
+        sa_sb = sb_tile("sa_sb", [P, PACK], F32)
+        nc.sync.dma_start(sa_sb[:], sa.rearrange("(p t) one -> p (t one)", t=PACK))
+        post_lists = [load_list("pw_list", offs4), load_list("pv_list", offs5), load_list("pu_list", offs6)]
+        place_list = load_list("place_list", offs7)
+        sb_sb = sb_tile("sb_sb", [P, PACK], F32)
+        nc.sync.dma_start(sb_sb[:], sb.rearrange("(p t) one -> p (t one)", t=PACK))
+        wb_sb = load_words("wb_sb", wb_words[0], 2 * N)
+        load_scale_rows(nc.sync, wb_plane, wb_scales)
+
+        xt_g = sb_tile("xt_g", [P, 2 * J], U8)
+        nc.vector.tensor_copy(xt_g[:].bitcast(U16), xt_table[:].bitcast(U16).indirect(tok_list[:]))
+        xt_gs = sb_tile("xt_gs", [P, J], U8)
+        nc.vector.tensor_copy(xt_gs[:], xt_plane[:].indirect(tok_list[:]))
+        xo_g = sb_tile("xo_g", [P, J], U32)
+        nc.vector.tensor_copy(xo_g[:], xo_table[:].bitcast(U32).indirect(note_list[:]))
+
+        w_dealt = sb_tile("w_dealt", [P, R], U32)
+        nc.scalar.copy(w_dealt[:].rearrange("p (t m) -> p m t", t=PACK), w_raw[:].bitcast(U32).rearrange("p (m t) -> p m t", t=PACK))
+        w2_dealt = sb_tile("w2_dealt", [P, 2 * R], U8)
+        nc.scalar.copy(
+            w2_dealt[:].bitcast(U16).rearrange("p (t m) -> p m t", t=PACK),
+            w2_raw[:].bitcast(U16).rearrange("p (m t) -> p m t", t=PACK),
+        )
+        for q in range(1, 4):
+            nc.vector.tensor_copy(w_stage[32 * q : 32 * q + 4, 0, :].bitcast(I32), w_stage[0:4, q, :].bitcast(I32))
+        scales_by_t = w_stage[:, 0, :].rearrange("p (w m t) -> p t w m", w=2, t=PACK)
+        ws_first = sb_tile("ws_first", [P, 2, P], U8)
+        nc.vector.tensor_copy(ws_first[:], scales_by_t[:, 0, :, :])
+
+        xo_gs = [sb_tile("xo_gs%d" % h, [P, HALF], U8) for h in range(2)]
+        for h in range(2):
+            nc.vector.tensor_copy(xo_gs[h][:], xo_plane[:].indirect(note_list[:, 16 * h : 16 * (h + 1)]))
+
+        def products(acc, t, h, ws, w2s):
+            cols = slice(HALF * h, HALF * (h + 1))
+            nc.tensor.matmul_mx(
+                acc, lhsT=w_dealt[:, P * t : P * (t + 1)].bitcast(FP8X4), lhsT_scale=ws,
+                rhs=xt_g[:, 2 * cols.start : 2 * cols.stop].bitcast(FP4X4), rhs_scale=xt_gs[:, cols], start=True, stop=False,
+            )
+            nc.tensor.matmul_mx(
+                acc, lhsT=w2_dealt[:, 2 * P * t : 2 * P * (t + 1)].bitcast(FP4X4), lhsT_scale=w2s,
+                rhs=xo_g[:, cols].bitcast(FP8X4), rhs_scale=xo_gs[h][:], start=False, stop=True,
+            )
+
+        a_sb = [sb_tile("a%d" % t, [P, J], F32) for t in range(PACK)]
+        for h in range(2):
+            acc = psum.tile([P, HALF], F32, name="acc0_%d" % h)
+            products(acc[:], 0, h, ws_first[:, 0, :], ws_first[:, 1, :])
+            nc.scalar.copy(a_sb[0][:, HALF * h : HALF * (h + 1)], acc[:])
+        ws_rest = sb_tile("ws_rest", [P, PACK - 1, 2, P], U8, tag="xo_plane")
+        nc.vector.tensor_copy(ws_rest[:], scales_by_t[:, 1:, :, :])
+        for t in range(1, PACK):
+            acc = psum.tile([P, J], F32, name="acc%d" % t)
+            for h in range(2):
+                products(acc[:, HALF * h : HALF * (h + 1)], t, h, ws_rest[:, t - 1, 0, :], ws_rest[:, t - 1, 1, :])
+            nc.vector.tensor_copy(a_sb[t][:], acc[:])
+
+        h1 = {}
+        g1 = {}
+
+        def fetch(t):
+            tag = "late" if t == PACK - 1 else "h1_%d" % (t % 2)
+            h1[t] = sb_tile("h1_%d" % t, [P, S], F32, tag=tag)
+            nc.scalar.activation(h1[t][:], a_sb[t][:].indirect(seat_list[:]), COPY, scale=sa_sb[:, t : t + 1])
+
+        def post(t, which):
+            nc.scalar.activation(boards[which][:].indirect(post_lists[which][:]), h1[t][:], COPY)
+
+        fetch(0)
+        for t in range(PACK):
+            post(t, 0)
+            post(t, 1)
+            total = sb_tile("total%d" % t, [P, C], F32, tag="total")
+            nc.vector.tensor_tensor(total[:], pw[:], pv[:], ALU.add)
+            if t + 1 < PACK:
+                fetch(t + 1)
+            post(t, 2)
+            diff = sb_tile("diff%d" % t, [P, C], F32, tag="diff")
+            g1[t] = sb_tile("g1_%d" % t, [P, C], F32)
+            for h in range(2):
+                cols = slice(HALF * h, HALF * (h + 1))
+                nc.vector.tensor_tensor(diff[:, cols], total[:, cols], pu[:, cols], ALU.subtract)
+            for h in range(2):
+                cols = slice(HALF * h, HALF * (h + 1))
+                nc.vector.tensor_scalar_max(g1[t][:, cols], diff[:, cols], 0.0)
+
+        hid = sb_tile("hid", [P, PACK, O], BF16, tag="late")
+        for t in range(PACK - 1):
+            nc.scalar.activation(hid[:, t, :], g1[t][:].indirect(place_list[:]), COPY, scale=sb_sb[:, t : t + 1])
+        last = PACK - 1
+        out_v = out.rearrange("(a p) o -> p a o", p=P)
+        for h in range(2):
+            cols = slice(P * h, P * (h + 1))
+            nc.scalar.activation(
+                hid[:, last, cols], g1[last][:].indirect(place_list[:, 8 * h : 8 * (h + 1)]), COPY, scale=sb_sb[:, last : last + 1]
+            )
+        grouped = [sb_tile("grouped%d" % h, [P, P, PACK], BF16) for h in range(2)]
+        for h in range(2):
+            cols = slice(P * h, P * (h + 1))
+            nc.vector.tensor_copy(
+                grouped[h][:].rearrange("p (c i) t -> p c t i", i=4), hid[:, :, cols].rearrange("p t (c i) -> p c t i", i=4)
+            )
+        for h in range(2):
+            cols = slice(P * h, P * (h + 1))
+            codes = sb_tile("codes%d" % h, [P, P], U32)
+            scales = sb_tile("scales%d" % h, [P, P], U8)
+            nc.vector.quantize_mx(codes[:].bitcast(FP8X4), scales[:], grouped[h][:].rearrange("p c t -> p (c t)"))
+            y = sb_tile("y%d" % h, [P, 2, P], F32)
+            for a in range(2):
+                acc = psum.tile([P, P], F32, name="y%d_%d" % (h, a), tag="acc%d" % (1 + a) if h == 0 else "acc0_%d" % a)
+                nc.tensor.matmul_mx(
+                    acc[:], lhsT=wb_sb[:, 2 * P * a : 2 * P * (a + 1)].bitcast(FP4X4), lhsT_scale=wb_plane[:, P * a : P * (a + 1)],
+                    rhs=codes[:].bitcast(FP8X4), rhs_scale=scales[:], start=True, stop=True,
+                )
+                if a == 0 or h == 0:
+                    nc.scalar.copy(y[:, a, :], acc[:])
+                else:
+                    nc.vector.tensor_copy(y[:, a, :], acc[:])
+            nc.sync.dma_start(out_v[:, :, cols], y[:])

@@ -17,6 +17,7 @@ K, J, R, T, Z, M, O, S, C, N = 512, 512, 512, 1024, 512, 1024, 256, 256, 512, 25
 P = 128
 PACK = 4
 HALF = 256
+PIECES = (slice(0, 256), slice(256, 384), slice(384, 512))
 FLOPS = 2 * (K * R * J + Z * R * J + R * N * O)
 
 
@@ -43,8 +44,8 @@ def tile_picked_tokens_plain_bank_threeposts_one_plain_kernel(
             nc.vector.memset(plane[:].bitcast(I32), 0)
             return plane
 
-        def load_scale_rows(queue, plane, src):
-            for q in range(4):
+        def load_scale_rows(queue, plane, src, quadrants=range(4)):
+            for q in quadrants:
                 queue.dma_start(plane[32 * q : 32 * q + 4, :].bitcast(I32), src[0, 4 * q : 4 * q + 4, :].bitcast(I32))
 
         def load_words(name, src, nbytes):
@@ -52,10 +53,9 @@ def tile_picked_tokens_plain_bank_threeposts_one_plain_kernel(
             nc.sync.dma_start(tile[:].bitcast(I32), src.bitcast(I32))
             return tile
 
-        xt_plane = zeroed_plane("xt_plane", T)
-        w_stage = sb_tile("w_stage", [P, 4, 2 * R], U8)
-        nc.vector.memset(w_stage[:, 0, :].bitcast(I32), 0)
         xo_plane = zeroed_plane("xo_plane", M)
+        xt_plane = zeroed_plane("xt_plane", T)
+        w_planes = zeroed_plane("w_planes", 4 * R)
         boards = []
         for name in ("pw", "pv", "pu"):
             board = sb_tile(name, [P, C], F32)
@@ -64,19 +64,23 @@ def tile_picked_tokens_plain_bank_threeposts_one_plain_kernel(
         pw, pv, pu = boards
         wb_plane = zeroed_plane("wb_plane", N)
 
+        def load_weight_scale_rows(queue, which, src):
+            blocks = w_planes[:].rearrange("p (b c) -> p b c", b=2)
+            rows = src[0].rearrange("(b q i) c -> q i b c", b=2, q=2)
+            for q in range(2):
+                queue.dma_start(blocks[32 * q : 32 * q + 4, :, R * which : R * (which + 1)].bitcast(I32), rows[q].bitcast(I32))
+
+        load_scale_rows(nc.gpsimd, xo_plane, xo_scales, range(2))
         tok_list = load_list("tok_list", offs)
         xt_table = load_words("xt_table", xt_words[0], 2 * T)
-        load_scale_rows(nc.sync, xt_plane, xt_scales)
         note_list = load_list("note_list", offs2)
         xo_table = load_words("xo_table", xo_words[0].rearrange("p c b -> p (c b)"), 4 * M)
-        for which, src in enumerate((w_scales, w2_scales)):
-            nc.sync.dma_start(
-                w_stage[0:4, :, R * which : R * (which + 1)].bitcast(I32),
-                src[0].rearrange("(q i) c -> i q c", i=4).bitcast(I32),
-            )
+        load_scale_rows(nc.sync, xt_plane, xt_scales)
         w_raw = load_words("w_raw", w_words[0].rearrange("p c b -> p (c b)"), 4 * R)
         w2_raw = load_words("w2_raw", w2_words[0], 2 * R)
-        load_scale_rows(nc.sync, xo_plane, xo_scales)
+        load_weight_scale_rows(nc.sync, 0, w_scales)
+        load_weight_scale_rows(nc.sync, 1, w2_scales)
+        load_scale_rows(nc.sync, xo_plane, xo_scales, range(2, 4))
         seat_list = load_list("seat_list", offs3)
         sa_sb = sb_tile("sa_sb", [P, PACK], F32)
         nc.sync.dma_start(sa_sb[:], sa.rearrange("(p t) one -> p (t one)", t=PACK))
@@ -89,10 +93,10 @@ def tile_picked_tokens_plain_bank_threeposts_one_plain_kernel(
 
         xt_g = sb_tile("xt_g", [P, 2 * J], U8)
         nc.vector.tensor_copy(xt_g[:].bitcast(U16), xt_table[:].bitcast(U16).indirect(tok_list[:]))
-        xt_gs = sb_tile("xt_gs", [P, J], U8)
-        nc.vector.tensor_copy(xt_gs[:], xt_plane[:].indirect(tok_list[:]))
         xo_g = sb_tile("xo_g", [P, J], U32)
         nc.vector.tensor_copy(xo_g[:], xo_table[:].bitcast(U32).indirect(note_list[:]))
+        xt_gs = sb_tile("xt_gs", [P, J], U8)
+        nc.vector.tensor_copy(xt_gs[:], xt_plane[:].indirect(tok_list[:]))
 
         w_dealt = sb_tile("w_dealt", [P, R], U32)
         nc.scalar.copy(w_dealt[:].rearrange("p (t m) -> p m t", t=PACK), w_raw[:].bitcast(U32).rearrange("p (m t) -> p m t", t=PACK))
@@ -101,45 +105,47 @@ def tile_picked_tokens_plain_bank_threeposts_one_plain_kernel(
             w2_dealt[:].bitcast(U16).rearrange("p (t m) -> p m t", t=PACK),
             w2_raw[:].bitcast(U16).rearrange("p (m t) -> p m t", t=PACK),
         )
-        for q in range(1, 4):
-            nc.vector.tensor_copy(w_stage[32 * q : 32 * q + 4, 0, :].bitcast(I32), w_stage[0:4, q, :].bitcast(I32))
-        scales_by_t = w_stage[:, 0, :].rearrange("p (w m t) -> p t w m", w=2, t=PACK)
+        nc.vector.tensor_copy(w_planes[64:128, 0 : 2 * R].bitcast(I32), w_planes[0:64, 2 * R : 4 * R].bitcast(I32))
+        scales_by_t = w_planes[:, 0 : 2 * R].rearrange("p (w m t) -> p t w m", w=2, t=PACK)
         ws_first = sb_tile("ws_first", [P, 2, P], U8)
         nc.vector.tensor_copy(ws_first[:], scales_by_t[:, 0, :, :])
 
-        xo_gs = [sb_tile("xo_gs%d" % h, [P, HALF], U8) for h in range(2)]
-        for h in range(2):
-            nc.vector.tensor_copy(xo_gs[h][:], xo_plane[:].indirect(note_list[:, 16 * h : 16 * (h + 1)]))
+        xo_gs = sb_tile("xo_gs", [P, J], U8)
+        for cols in PIECES:
+            nc.vector.tensor_copy(xo_gs[:, cols], xo_plane[:].indirect(note_list[:, cols.start // 16 : cols.stop // 16]))
 
-        def products(acc, t, h, ws, w2s):
-            cols = slice(HALF * h, HALF * (h + 1))
+        def token_pass(acc, t, cols, ws):
             nc.tensor.matmul_mx(
                 acc, lhsT=w_dealt[:, P * t : P * (t + 1)].bitcast(FP8X4), lhsT_scale=ws,
                 rhs=xt_g[:, 2 * cols.start : 2 * cols.stop].bitcast(FP4X4), rhs_scale=xt_gs[:, cols], start=True, stop=False,
             )
+
+        def note_pass(acc, t, cols, w2s):
             nc.tensor.matmul_mx(
                 acc, lhsT=w2_dealt[:, 2 * P * t : 2 * P * (t + 1)].bitcast(FP4X4), lhsT_scale=w2s,
-                rhs=xo_g[:, cols].bitcast(FP8X4), rhs_scale=xo_gs[h][:], start=False, stop=True,
+                rhs=xo_g[:, cols].bitcast(FP8X4), rhs_scale=xo_gs[:, cols], start=False, stop=True,
             )
 
         a_sb = [sb_tile("a%d" % t, [P, J], F32) for t in range(PACK)]
-        for h in range(2):
-            acc = psum.tile([P, HALF], F32, name="acc0_%d" % h)
-            products(acc[:], 0, h, ws_first[:, 0, :], ws_first[:, 1, :])
-            nc.scalar.copy(a_sb[0][:, HALF * h : HALF * (h + 1)], acc[:])
+        first = [psum.tile([P, cols.stop - cols.start], F32, name="acc0_%d" % i) for i, cols in enumerate(PIECES)]
+        for acc, cols in zip(first, PIECES):
+            token_pass(acc[:], 0, cols, ws_first[:, 0, :])
+        for acc, cols in zip(first, PIECES):
+            note_pass(acc[:], 0, cols, ws_first[:, 1, :])
+            nc.scalar.copy(a_sb[0][:, cols], acc[:])
         ws_rest = sb_tile("ws_rest", [P, PACK - 1, 2, P], U8, tag="xo_plane")
         nc.vector.tensor_copy(ws_rest[:], scales_by_t[:, 1:, :, :])
         for t in range(1, PACK):
             acc = psum.tile([P, J], F32, name="acc%d" % t)
-            for h in range(2):
-                products(acc[:, HALF * h : HALF * (h + 1)], t, h, ws_rest[:, t - 1, 0, :], ws_rest[:, t - 1, 1, :])
+            token_pass(acc[:], t, slice(0, J), ws_rest[:, t - 1, 0, :])
+            note_pass(acc[:], t, slice(0, J), ws_rest[:, t - 1, 1, :])
             nc.vector.tensor_copy(a_sb[t][:], acc[:])
 
         h1 = {}
         g1 = {}
 
         def fetch(t):
-            tag = "late" if t == PACK - 1 else "h1_%d" % (t % 2)
+            tag = "h1_%d" % (t % 2)
             h1[t] = sb_tile("h1_%d" % t, [P, S], F32, tag=tag)
             nc.scalar.activation(h1[t][:], a_sb[t][:].indirect(seat_list[:]), COPY, scale=sa_sb[:, t : t + 1])
 
@@ -164,7 +170,7 @@ def tile_picked_tokens_plain_bank_threeposts_one_plain_kernel(
                 cols = slice(HALF * h, HALF * (h + 1))
                 nc.vector.tensor_scalar_max(g1[t][:, cols], diff[:, cols], 0.0)
 
-        hid = sb_tile("hid", [P, PACK, O], BF16, tag="late")
+        hid = sb_tile("hid", [P, PACK, O], BF16, tag="pw")
         for t in range(PACK - 1):
             nc.scalar.activation(hid[:, t, :], g1[t][:].indirect(place_list[:]), COPY, scale=sb_sb[:, t : t + 1])
         last = PACK - 1

@@ -29,6 +29,7 @@ def tile_picked_tokens_plain_bank_threeposts_one_plain_kernel(
     with ExitStack() as ctx:
         lists = ctx.enter_context(tc.tile_pool(name="lists", bufs=1))
         keep = ctx.enter_context(tc.tile_pool(name="keep", bufs=1))
+        shared = ctx.enter_context(tc.tile_pool(name="shared", bufs=1))
         psum = ctx.enter_context(tc.psum_pool(name="psum", bufs=1))
 
         def sb_tile(name, shape, dtype, **kw):
@@ -53,15 +54,10 @@ def tile_picked_tokens_plain_bank_threeposts_one_plain_kernel(
             nc.sync.dma_start(tile[:].bitcast(I32), src.bitcast(I32))
             return tile
 
-        xo_plane = zeroed_plane("xo_plane", M)
+        xo_plane = shared.tile([P, M], U8, name="xo_plane", align_bytes=64, offset=4 * C - M // 2)
+        nc.vector.memset(xo_plane[:].bitcast(I32), 0)
         xt_plane = zeroed_plane("xt_plane", T)
         w_planes = zeroed_plane("w_planes", 4 * R)
-        boards = []
-        for name in ("pw", "pv", "pu"):
-            board = sb_tile(name, [P, C], F32)
-            nc.vector.memset(board[:], 0.0)
-            boards.append(board)
-        pw, pv, pu = boards
         wb_plane = zeroed_plane("wb_plane", N)
 
         def load_weight_scale_rows(queue, which, src):
@@ -71,8 +67,8 @@ def tile_picked_tokens_plain_bank_threeposts_one_plain_kernel(
                 queue.dma_start(blocks[32 * q : 32 * q + 4, :, R * which : R * (which + 1)].bitcast(I32), rows[q].bitcast(I32))
 
         load_scale_rows(nc.gpsimd, xo_plane, xo_scales, range(2))
-        tok_list = load_list("tok_list", offs)
         xt_table = load_words("xt_table", xt_words[0], 2 * T)
+        tok_list = load_list("tok_list", offs)
         note_list = load_list("note_list", offs2)
         xo_table = load_words("xo_table", xo_words[0].rearrange("p c b -> p (c b)"), 4 * M)
         load_scale_rows(nc.sync, xt_plane, xt_scales)
@@ -133,8 +129,15 @@ def tile_picked_tokens_plain_bank_threeposts_one_plain_kernel(
         for acc, cols in zip(first, PIECES):
             note_pass(acc[:], 0, cols, ws_first[:, 1, :])
             nc.scalar.copy(a_sb[0][:, cols], acc[:])
-        ws_rest = sb_tile("ws_rest", [P, PACK - 1, 2, P], U8, tag="xo_plane")
+        pw = shared.tile([P, C], F32, name="pw", align_bytes=64, offset=0)
+        nc.vector.memset(pw[:], 0.0)
+        ws_rest = sb_tile("ws_rest", [P, PACK - 1, 2, P], U8, tag="ws_first")
         nc.vector.tensor_copy(ws_rest[:], scales_by_t[:, 1:, :, :])
+        pv = sb_tile("pv", [P, C], F32, tag="w_planes")
+        nc.vector.memset(pv[:], 0.0)
+        pu = shared.tile([P, C], F32, name="pu", align_bytes=64, offset=4 * C)
+        nc.vector.memset(pu[:], 0.0)
+        boards = [pw, pv, pu]
         for t in range(1, PACK):
             acc = psum.tile([P, J], F32, name="acc%d" % t)
             token_pass(acc[:], t, slice(0, J), ws_rest[:, t - 1, 0, :])
@@ -170,7 +173,7 @@ def tile_picked_tokens_plain_bank_threeposts_one_plain_kernel(
                 cols = slice(HALF * h, HALF * (h + 1))
                 nc.vector.tensor_scalar_max(g1[t][:, cols], diff[:, cols], 0.0)
 
-        hid = sb_tile("hid", [P, PACK, O], BF16, tag="pw")
+        hid = shared.tile([P, PACK, O], BF16, name="hid", tag="pw", align_bytes=64, offset=0)
         for t in range(PACK - 1):
             nc.scalar.activation(hid[:, t, :], g1[t][:].indirect(place_list[:]), COPY, scale=sb_sb[:, t : t + 1])
         last = PACK - 1

from contextlib import ExitStack

import concourse.mybir as mybir

F32 = mybir.dt.float32
BF16 = mybir.dt.bfloat16
I32 = mybir.dt.int32
U32 = mybir.dt.uint32
U16 = mybir.dt.uint16
U8 = mybir.dt.uint8
FP8X4 = mybir.dt.float8_e4m3fn_x4
FP4X4 = mybir.dt.float4_e2m1fn_x4
ALU = mybir.AluOpType
COPY = mybir.ActivationFunctionType.Copy

K, J, R, T, Z, M, O, S, C, N = 512, 512, 512, 1024, 512, 1024, 256, 256, 512, 256
P = 128
PACK = 4
HALF = 256
PIECES = (slice(0, 256), slice(256, 384), slice(384, 512))
FLOPS = 2 * (K * R * J + Z * R * J + R * N * O)


def tile_picked_tokens_plain_bank_threeposts_one_plain_kernel(
    tc, xt_words, xt_scales, w_words, w_scales, xo_words, xo_scales, w2_words, w2_scales, sa, sb,
    wb_words, wb_scales, offs, offs2, offs3, offs4, offs5, offs6, offs7, out,
):
    nc = tc.nc
    with ExitStack() as ctx:
        lists = ctx.enter_context(tc.tile_pool(name="lists", bufs=1))
        keep = ctx.enter_context(tc.tile_pool(name="keep", bufs=1))
        shared = ctx.enter_context(tc.tile_pool(name="shared", bufs=1))
        psum = ctx.enter_context(tc.psum_pool(name="psum", bufs=1))

        def sb_tile(name, shape, dtype, **kw):
            return keep.tile(shape, dtype, name=name, align_bytes=64, **kw)

        def load_list(name, src):
            tile = lists.tile(list(src.shape), U16, name=name)
            nc.sync.dma_start(tile[:], src)
            return tile

        def zeroed_plane(name, width):
            plane = sb_tile(name, [P, width], U8)
            nc.vector.memset(plane[:].bitcast(I32), 0)
            return plane

        def load_scale_rows(queue, plane, src, quadrants=range(4)):
            for q in quadrants:
                queue.dma_start(plane[32 * q : 32 * q + 4, :].bitcast(I32), src[0, 4 * q : 4 * q + 4, :].bitcast(I32))

        def load_words(name, src, nbytes):
            tile = sb_tile(name, [P, nbytes], U8)
            nc.sync.dma_start(tile[:].bitcast(I32), src.bitcast(I32))
            return tile

        xo_plane = shared.tile([P, M], U8, name="xo_plane", align_bytes=64, offset=4 * C - M // 2)
        nc.vector.memset(xo_plane[:].bitcast(I32), 0)
        xt_plane = zeroed_plane("xt_plane", T)
        w_planes = zeroed_plane("w_planes", 4 * R)
        wb_plane = zeroed_plane("wb_plane", N)

        def load_weight_scale_rows(queue, which, src):
            blocks = w_planes[:].rearrange("p (b c) -> p b c", b=2)
            rows = src[0].rearrange("(b q i) c -> q i b c", b=2, q=2)
            for q in range(2):
                queue.dma_start(blocks[32 * q : 32 * q + 4, :, R * which : R * (which + 1)].bitcast(I32), rows[q].bitcast(I32))

        load_scale_rows(nc.gpsimd, xo_plane, xo_scales, range(2))
        xt_table = load_words("xt_table", xt_words[0], 2 * T)
        tok_list = load_list("tok_list", offs)
        note_list = load_list("note_list", offs2)
        xo_table = load_words("xo_table", xo_words[0].rearrange("p c b -> p (c b)"), 4 * M)
        load_scale_rows(nc.sync, xt_plane, xt_scales)
        w_raw = load_words("w_raw", w_words[0].rearrange("p c b -> p (c b)"), 4 * R)
        w2_raw = load_words("w2_raw", w2_words[0], 2 * R)
        load_weight_scale_rows(nc.sync, 0, w_scales)
        load_weight_scale_rows(nc.sync, 1, w2_scales)
        load_scale_rows(nc.sync, xo_plane, xo_scales, range(2, 4))
        seat_list = load_list("seat_list", offs3)
        sa_sb = sb_tile("sa_sb", [P, PACK], F32)
        nc.sync.dma_start(sa_sb[:], sa.rearrange("(p t) one -> p (t one)", t=PACK))
        post_lists = [load_list("pw_list", offs4), load_list("pv_list", offs5), load_list("pu_list", offs6)]
        place_list = load_list("place_list", offs7)
        sb_sb = sb_tile("sb_sb", [P, PACK], F32)
        nc.sync.dma_start(sb_sb[:], sb.rearrange("(p t) one -> p (t one)", t=PACK))
        wb_sb = load_words("wb_sb", wb_words[0], 2 * N)
        load_scale_rows(nc.sync, wb_plane, wb_scales)

        xt_g = sb_tile("xt_g", [P, 2 * J], U8)
        nc.vector.tensor_copy(xt_g[:].bitcast(U16), xt_table[:].bitcast(U16).indirect(tok_list[:]))
        xo_g = sb_tile("xo_g", [P, J], U32)
        nc.vector.tensor_copy(xo_g[:], xo_table[:].bitcast(U32).indirect(note_list[:]))
        xt_gs = sb_tile("xt_gs", [P, J], U8)
        nc.vector.tensor_copy(xt_gs[:], xt_plane[:].indirect(tok_list[:]))

        w_dealt = sb_tile("w_dealt", [P, R], U32)
        nc.scalar.copy(w_dealt[:].rearrange("p (t m) -> p m t", t=PACK), w_raw[:].bitcast(U32).rearrange("p (m t) -> p m t", t=PACK))
        w2_dealt = sb_tile("w2_dealt", [P, 2 * R], U8)
        nc.scalar.copy(
            w2_dealt[:].bitcast(U16).rearrange("p (t m) -> p m t", t=PACK),
            w2_raw[:].bitcast(U16).rearrange("p (m t) -> p m t", t=PACK),
        )
        nc.vector.tensor_copy(w_planes[64:128, 0 : 2 * R].bitcast(I32), w_planes[0:64, 2 * R : 4 * R].bitcast(I32))
        scales_by_t = w_planes[:, 0 : 2 * R].rearrange("p (w m t) -> p t w m", w=2, t=PACK)
        ws_first = sb_tile("ws_first", [P, 2, P], U8)
        nc.vector.tensor_copy(ws_first[:], scales_by_t[:, 0, :, :])

        xo_gs = sb_tile("xo_gs", [P, J], U8)
        for cols in PIECES:
            nc.vector.tensor_copy(xo_gs[:, cols], xo_plane[:].indirect(note_list[:, cols.start // 16 : cols.stop // 16]))

        def token_pass(acc, t, cols, ws):
            nc.tensor.matmul_mx(
                acc, lhsT=w_dealt[:, P * t : P * (t + 1)].bitcast(FP8X4), lhsT_scale=ws,
                rhs=xt_g[:, 2 * cols.start : 2 * cols.stop].bitcast(FP4X4), rhs_scale=xt_gs[:, cols], start=True, stop=False,
            )

        def note_pass(acc, t, cols, w2s):
            nc.tensor.matmul_mx(
                acc, lhsT=w2_dealt[:, 2 * P * t : 2 * P * (t + 1)].bitcast(FP4X4), lhsT_scale=w2s,
                rhs=xo_g[:, cols].bitcast(FP8X4), rhs_scale=xo_gs[:, cols], start=False, stop=True,
            )

        a_sb = [sb_tile("a%d" % t, [P, J], F32) for t in range(PACK)]
        first = [psum.tile([P, cols.stop - cols.start], F32, name="acc0_%d" % i) for i, cols in enumerate(PIECES)]
        for acc, cols in zip(first, PIECES):
            token_pass(acc[:], 0, cols, ws_first[:, 0, :])
        for acc, cols in zip(first, PIECES):
            note_pass(acc[:], 0, cols, ws_first[:, 1, :])
            nc.scalar.copy(a_sb[0][:, cols], acc[:])
        pw = shared.tile([P, C], F32, name="pw", align_bytes=64, offset=0)
        nc.vector.memset(pw[:], 0.0)
        ws_rest = sb_tile("ws_rest", [P, PACK - 1, 2, P], U8, tag="ws_first")
        nc.vector.tensor_copy(ws_rest[:], scales_by_t[:, 1:, :, :])
        pv = sb_tile("pv", [P, C], F32, tag="w_planes")
        nc.vector.memset(pv[:], 0.0)
        pu = shared.tile([P, C], F32, name="pu", align_bytes=64, offset=4 * C)
        nc.vector.memset(pu[:], 0.0)
        boards = [pw, pv, pu]
        for t in range(1, PACK):
            acc = psum.tile([P, J], F32, name="acc%d" % t)
            token_pass(acc[:], t, slice(0, J), ws_rest[:, t - 1, 0, :])
            note_pass(acc[:], t, slice(0, J), ws_rest[:, t - 1, 1, :])
            nc.vector.tensor_copy(a_sb[t][:], acc[:])

        h1 = {}
        g1 = {}

        def fetch(t):
            tag = "h1_%d" % (t % 2)
            h1[t] = sb_tile("h1_%d" % t, [P, S], F32, tag=tag)
            nc.scalar.activation(h1[t][:], a_sb[t][:].indirect(seat_list[:]), COPY, scale=sa_sb[:, t : t + 1])

        def post(t, which):
            nc.scalar.activation(boards[which][:].indirect(post_lists[which][:]), h1[t][:], COPY)

        fetch(0)
        for t in range(PACK):
            post(t, 0)
            post(t, 1)
            total = sb_tile("total%d" % t, [P, C], F32, tag="total")
            nc.vector.tensor_tensor(total[:], pw[:], pv[:], ALU.add)
            if t + 1 < PACK:
                fetch(t + 1)
            post(t, 2)
            diff = sb_tile("diff%d" % t, [P, C], F32, tag="diff")
            g1[t] = sb_tile("g1_%d" % t, [P, C], F32)
            for h in range(2):
                cols = slice(HALF * h, HALF * (h + 1))
                nc.vector.tensor_tensor(diff[:, cols], total[:, cols], pu[:, cols], ALU.subtract)
            for h in range(2):
                cols = slice(HALF * h, HALF * (h + 1))
                nc.vector.tensor_scalar_max(g1[t][:, cols], diff[:, cols], 0.0)

        hid = shared.tile([P, PACK, O], BF16, name="hid", tag="pw", align_bytes=64, offset=0)
        for t in range(PACK - 1):
            nc.scalar.activation(hid[:, t, :], g1[t][:].indirect(place_list[:]), COPY, scale=sb_sb[:, t : t + 1])
        last = PACK - 1
        out_v = out.rearrange("(a p) o -> p a o", p=P)
        for h in range(2):
            cols = slice(P * h, P * (h + 1))
            nc.scalar.activation(
                hid[:, last, cols], g1[last][:].indirect(place_list[:, 8 * h : 8 * (h + 1)]), COPY, scale=sb_sb[:, last : last + 1]
            )
        grouped = [sb_tile("grouped%d" % h, [P, P, PACK], BF16) for h in range(2)]
        for h in range(2):
            cols = slice(P * h, P * (h + 1))
            nc.vector.tensor_copy(
                grouped[h][:].rearrange("p (c i) t -> p c t i", i=4), hid[:, :, cols].rearrange("p t (c i) -> p c t i", i=4)
            )
        for h in range(2):
            cols = slice(P * h, P * (h + 1))
            codes = sb_tile("codes%d" % h, [P, P], U32)
            scales = sb_tile("scales%d" % h, [P, P], U8)
            nc.vector.quantize_mx(codes[:].bitcast(FP8X4), scales[:], grouped[h][:].rearrange("p c t -> p (c t)"))
            y = sb_tile("y%d" % h, [P, 2, P], F32)
            for a in range(2):
                acc = psum.tile([P, P], F32, name="y%d_%d" % (h, a), tag="acc%d" % (1 + a) if h == 0 else "acc0_%d" % a)
                nc.tensor.matmul_mx(
                    acc[:], lhsT=wb_sb[:, 2 * P * a : 2 * P * (a + 1)].bitcast(FP4X4), lhsT_scale=wb_plane[:, P * a : P * (a + 1)],
                    rhs=codes[:].bitcast(FP8X4), rhs_scale=scales[:], start=True, stop=True,
                )
                if a == 0 or h == 0:
                    nc.scalar.copy(y[:, a, :], acc[:])
                else:
                    nc.vector.tensor_copy(y[:, a, :], acc[:])
            nc.sync.dma_start(out_v[:, :, cols], y[:])
